import numpy as np
import ml_dtypes


def mxq(x, axis, fmt="e4m3"):
    dtype, down = {"e4m3": (ml_dtypes.float8_e4m3fn, 7), "e5m2": (ml_dtypes.float8_e5m2, 14)}[fmt]
    v = np.moveaxis(np.asarray(x, np.float32).astype(ml_dtypes.bfloat16).astype(np.float64), axis, -1)
    blocks = v.reshape(v.shape[:-1] + (-1, 32))
    amax = np.abs(blocks).max(-1, keepdims=True)
    byte = np.maximum(np.where(amax > 0, np.frexp(amax)[1] - 1 + 127, 0) - down, 1)
    scale = np.exp2(byte - 127.0)
    codes = (blocks / scale).astype(np.float32).astype(dtype).astype(np.float64)
    return np.moveaxis((codes * scale).reshape(v.shape), -1, axis)


WIDE = False


def mx_kscale(k):
    if not WIDE:
        return np.ones(k)
    levels = np.array([10, -10, 5, -5, 0])
    if k % 512:
        return np.exp2(np.random.permutation(np.resize(levels, k // 32))).repeat(32)
    a = np.empty((k // 512, 16))
    for p in range(k // 512):
        a[p, :8] = np.random.permutation(np.resize(levels, 8))
        for g in range(8):
            far = levels[np.abs(levels - a[p, g]) >= 10]
            a[p, g + 8] = far[np.random.randint(len(far))]
    return np.exp2(a.ravel()).repeat(32)


def f64(x):
    return np.asarray(x).astype(np.float64)


def striped(idx):
    return np.tile(idx.reshape(-1, 16).T, (8, 1)).astype(np.uint16)


def unstriped(offs):
    return offs[:16].T.reshape(-1).astype(np.int64)


def striped8(idx):
    return np.concatenate([x.reshape(-1, 16).T for x in idx]).astype(np.uint16)


def runs(offs, k):
    lists = np.stack([offs[16 * r : 16 * r + 16].T.reshape(-1) for r in range(8)]).astype(np.int64)
    return lists[np.arange(k) % 512 // 64]


def pack_weight(w):
    k, n = w.shape
    w = f64(np.asarray(w, np.float32).astype(ml_dtypes.bfloat16)).reshape(k // 32, 32, n)
    amax = np.abs(w).max(1)
    byte = np.clip(np.where(amax > 0, np.frexp(amax)[1] - 1 + 127 - 7, 1), 1, 254)
    scaled = (w * np.exp2(127.0 - byte)[:, None, :]).reshape(k, n).astype(np.float32)
    words = np.ascontiguousarray(scaled.reshape(k // 512, 128, 4, n).transpose(0, 1, 3, 2)).astype(ml_dtypes.float8_e4m3fn).view(np.uint8)
    return words, np.ascontiguousarray(byte.astype(np.uint8).reshape(k // 512, 16, n))


def unpack_weight(words, scales):
    g, p, n, _ = words.shape
    vals = np.ascontiguousarray(words).view(ml_dtypes.float8_e4m3fn).astype(np.float64) * np.repeat(np.exp2(scales.astype(np.float64) - 127.0), 8, axis=1)[..., None]
    return vals.transpose(0, 1, 3, 2).reshape(g * 512, n)

def planes(y):
    n, m = y.shape
    v = y.astype(np.float32).astype(ml_dtypes.bfloat16).astype(np.float64).reshape(n // 32, 32, m)
    top = np.abs(v).max(1)
    byte = np.clip(np.where(top > 0, np.frexp(top)[1] - 1 + 127 - 7, 1), 1, 254)
    codes = (v * np.exp2(127.0 - byte)[:, None, :]).reshape(n, m).astype(np.float32).astype(ml_dtypes.float8_e4m3fn).view(np.uint8)
    words = codes.reshape(n // 512, 128, 4, m).transpose(0, 1, 3, 2)
    return np.ascontiguousarray(words), np.ascontiguousarray(byte.astype(np.uint8).reshape(n // 512, 16, m))


K, T, S, N, H, W = 512, 2048, 512, 512, 512, 256


def setup_inputs():
    n = np.random.standard_normal
    s = mx_kscale(K)[:, None]
    u = mx_kscale(S)
    packed_xT = pack_weight(n((K, T)) * s)
    perm = np.stack([np.random.permutation(H) for _ in range(8)])
    return {
        "x_words": packed_xT[0],
        "x_scales": packed_xT[1],
        "wa": (n((K, H)) / np.sqrt(K) / s).astype(np.float32),
        "wb": (n((K, N)) / np.sqrt(K) / s).astype(np.float32),
        "gt": (np.random.uniform(0.5, 1.5, (S, 1)) * u[:, None]).astype(np.float32),
        "gi": (np.random.uniform(0.5, 1.5, (S, 1)) / u[:, None]).astype(np.float32),
        "offs": striped(np.random.permutation(T)[:S]),
        "two": striped(np.random.permutation(T)[:S]),
        "n1": striped8(perm[:, :W]),
        "n2": striped8(perm[:, W:]),
        "n3": striped8(np.stack([np.random.permutation(N) for _ in range(8)])),
        "n4": striped8(np.stack([np.random.permutation(N) for _ in range(8)])),
        "n5": striped8(np.stack([np.random.permutation(N) for _ in range(8)])),
        "n6": striped8(np.stack([np.random.permutation(N) for _ in range(8)])),
    }


def reference(x_words, x_scales, wa, wb, gt, gi, offs, two, n1, n2, n3, n4, n5, n6):
    xq = unpack_weight(x_words, x_scales)[:, unstriped(offs)]
    a = xq.T @ mxq(f64(wa), 0, "e4m3")
    pa = a[np.arange(S)[:, None], runs(n1, S)]
    pb = a[np.arange(S)[:, None], runs(n2, S)]
    rb = np.maximum(0.5 * pa, pb)
    ra = pb - pa
    ds = np.zeros((S, H))
    ds[np.arange(S)[:, None], runs(n1, S)] = ra
    dt = ds.copy()
    dt[np.arange(S)[:, None], runs(n2, S)] = rb
    z = f64(gt) * dt
    x_two = unpack_weight(x_words, x_scales)[:, unstriped(two)]
    b = x_two.T @ mxq(f64(wb), 0, "e4m3")
    z2 = f64(gi) * ((b - (b[np.arange(S)[:, None], runs(n3, S)])) / (np.abs(b[np.arange(S)[:, None], runs(n4, S)] - b) + 0.5))
    cv = 0.0625 * ((mxq(z, 0, "e4m3").T @ mxq(z2, 0, "e4m3")))
    out_0 = np.minimum(np.maximum(cv, cv[np.arange(H)[:, None], runs(n5, H)]), cv[np.arange(H)[:, None], runs(n6, H)])
    return (out_0,) + planes(out_0)

@@ -1,0 +1,289 @@
+from contextlib import ExitStack
+
+import concourse.mybir as mybir
+from concourse.masks import make_identity
+
+K, T, S, N, H, W = 512, 2048, 512, 512, 512, 256
+FLOPS = 2 * K * S * H + 2 * K * S * N + 2 * S * H * N
+
+F32 = mybir.dt.float32
+BF16 = mybir.dt.bfloat16
+I32 = mybir.dt.int32
+U32 = mybir.dt.uint32
+U16 = mybir.dt.uint16
+U8 = mybir.dt.uint8
+FP8X4 = mybir.dt.float8_e4m3fn_x4
+ALU = mybir.AluOpType
+ACT = mybir.ActivationFunctionType
+
+P = 128
+PACK = 4
+HALF = 256
+RUN = 4
+PER_COL = 16
+
+
+def tile_picked_mombliftfracminmx_none_po_kernel(
+    tc, x_words, x_scales, wa, wb, gt, gi, offs, two, n1, n2, n3, n4, n5, n6, out_0, out_1, out_2
+):
+    nc = tc.nc
+    with ExitStack() as ctx:
+        held = ctx.enter_context(tc.tile_pool(name="held", bufs=1))
+        keep = ctx.enter_context(tc.tile_pool(name="keep", bufs=1))
+        psum = ctx.enter_context(tc.psum_pool(name="psum", bufs=1))
+
+        def load_list(src, name):
+            tile = held.tile(list(src.shape), U16, name=name)
+            nc.sync.dma_start(tile[:], src)
+            return tile
+
+        def sb(shape, dtype, name):
+            return keep.tile(shape, dtype, name=name, align_bytes=64)
+
+        def bank(j):
+            return psum.tile([P, 512], F32, name="bank", tag="bank%d" % j)
+
+        def cols(h):
+            return slice(h * HALF, (h + 1) * HALF)
+
+        def entries(tile, h):
+            return tile[:, h * HALF // PER_COL : (h + 1) * HALF // PER_COL]
+
+        def woven(ap):
+            return ap.rearrange("p (c i t) -> p c t i", i=RUN, t=PACK)
+
+        def planes(ap):
+            return ap.rearrange("p t (c i) -> p c t i", i=RUN)
+
+        offs_t = load_list(offs, "offs_t")
+        xw = sb([P, T], I32, "xw")
+        nc.sync.dma_start(xw[:], x_words[0].rearrange("p n t -> p (n t)").bitcast(I32))
+        xs = sb([P, T], U8, "xs")
+        nc.vector.memset(xs[:].bitcast(I32), 0)
+        for q in range(4):
+            nc.scalar.dma_start(xs[32 * q : 32 * q + 4, :].bitcast(I32), x_scales[0, 4 * q : 4 * q + 4, :].bitcast(I32))
+        two_t = load_list(two, "two_t")
+        wa_rows = wa.rearrange("(p j) c -> p j c", j=PACK)
+        wa_raw = [sb([P, PACK, HALF], F32, "wa_raw%d" % h) for h in range(2)]
+        for h in range(2):
+            nc.sync.dma_start(wa_raw[h][:], wa_rows[:, :, cols(h)])
+        n1_t = load_list(n1, "n1_t")
+        n2_t = load_list(n2, "n2_t")
+        wb_raw = sb([P, PACK, N], F32, "wb_raw")
+        nc.sync.dma_start(wb_raw[:], wb.rearrange("(p j) c -> p j c", j=PACK))
+        g_rows = sb([P, P], F32, "g_rows")
+        nc.gpsimd.memset(g_rows[:], 0.0)
+        ident = sb([P, P], F32, "ident")
+        make_identity(nc, ident[:])
+        for j, g in enumerate((gt, gi)):
+            nc.sync.dma_start(
+                g_rows[PACK * j : PACK * (j + 1), :].rearrange("t (c b) -> t c b", b=4),
+                g.rearrange("(c t b) o -> t c (b o)", t=PACK, b=4),
+            )
+        n4_t = load_list(n4, "n4_t")
+        n3_t = load_list(n3, "n3_t")
+        n5_t = load_list(n5, "n5_t")
+        n6_t = load_list(n6, "n6_t")
+
+        def pick_words(lst, name):
+            words = sb([P, S], U32, name)
+            nc.vector.tensor_copy(
+                words[:].rearrange("p (t c b) -> p c t b", t=PACK, b=4), xw[:].bitcast(U32).indirect(lst[:])
+            )
+            return words
+
+        def pick_scales(lst, name):
+            raw = sb([P, S], U8, name + "_raw")
+            nc.vector.tensor_copy(raw[:], xs[:].indirect(lst[:]))
+            dealt = sb([P, S], U8, name)
+            nc.vector.tensor_copy(
+                dealt[:].bitcast(I32).rearrange("p (t c) -> p t c", t=PACK),
+                raw[:].bitcast(I32).rearrange("p (c t) -> p t c", t=PACK),
+            )
+            return dealt
+
+        def quantise(codes, scales, grouped):
+            nc.vector.quantize_mx(out=codes.bitcast(FP8X4), scales=scales, in_=grouped)
+
+        def product(out, lhs_codes, lhs_scales, rhs_codes, rhs_scales):
+            nc.tensor.matmul_mx(
+                out=out,
+                lhsT=lhs_codes.bitcast(FP8X4),
+                lhsT_scale=lhs_scales,
+                rhs=rhs_codes.bitcast(FP8X4),
+                rhs_scale=rhs_scales,
+                start=True,
+                stop=True,
+            )
+
+        xa_words = pick_words(offs_t, "xa_words")
+        xb_words = pick_words(two_t, "xb_words")
+        xa_scales = pick_scales(offs_t, "xa_scales")
+
+        wa_bf = [sb([P, HALF * PACK], BF16, "wa_bf%d" % h) for h in range(2)]
+        wa_codes = sb([P, H], U32, "wa_codes")
+        wa_scales = sb([P, H], U8, "wa_scales")
+        for h in range(2):
+            nc.scalar.copy(woven(wa_bf[h][:]), planes(wa_raw[h][:]))
+            quantise(wa_codes[:, cols(h)], wa_scales[:, cols(h)], wa_bf[h][:])
+        xb_scales = pick_scales(two_t, "xb_scales")
+
+        a_rows = [sb([P, H], F32, "a_rows%d" % t) for t in range(PACK)]
+        for t in range(PACK):
+            acc = bank(t)
+            tok = slice(t * P, (t + 1) * P)
+            product(acc[:], xa_words[:, tok], xa_scales[:, tok], wa_codes[:], wa_scales[:])
+            nc.scalar.copy(a_rows[t][:], acc[:])
+
+        g_ps = bank(PACK)
+        nc.tensor.transpose(g_ps[:, 0:P], g_rows[:], ident[:])
+        g_cols = sb([P, 2 * PACK], F32, "g_cols")
+        nc.scalar.copy(g_cols[:], g_ps[:, 0 : 2 * PACK])
+        gi_neg = sb([P, PACK], F32, "gi_neg")
+        nc.scalar.activation(gi_neg[:], g_ps[:, PACK : 2 * PACK], ACT.Copy, scale=-1.0)
+        gi_safe = sb([P, PACK], F32, "gi_safe")
+        gi_inv = sb([P, PACK], F32, "gi_inv")
+
+        neg_half = [sb([P, W], F32, "neg_half%d" % t) for t in range(PACK)]
+        pos_half = [sb([P, W], F32, "pos_half%d" % t) for t in range(PACK)]
+        excess = [sb([P, W], F32, "excess%d" % t) for t in range(PACK)]
+        over = [sb([P, W], F32, "over%d" % t) for t in range(PACK)]
+        dt = [sb([P, H], F32, "dt%d" % t) for t in range(PACK)]
+        z_dealt = sb([P, PACK, H], F32, "z_dealt")
+
+        def lift_gather_first(t):
+            nc.vector.tensor_scalar(neg_half[t][:], a_rows[t][:].indirect(n1_t[:]), -0.5, 0.0, ALU.mult, ALU.add)
+            nc.scalar.activation(pos_half[t][:], neg_half[t][:], ACT.Copy, scale=-1.0)
+
+        def lift_gather_second(t):
+            nc.vector.tensor_tensor(excess[t][:], a_rows[t][:].indirect(n2_t[:]), neg_half[t][:], ALU.add)
+            nc.scalar.activation(over[t][:], excess[t][:], ACT.Relu)
+
+        def lift_scatter_first(t):
+            nc.vector.tensor_tensor(dt[t][:].indirect(n1_t[:]), excess[t][:], neg_half[t][:], ALU.add)
+
+        def lift_scatter_second(t):
+            nc.vector.tensor_tensor(dt[t][:].indirect(n2_t[:]), over[t][:], pos_half[t][:], ALU.add)
+            nc.scalar.activation(
+                z_dealt[:, t, :].rearrange("p (u m) -> p m u", u=PACK),
+                dt[t][:].rearrange("p (m u) -> p m u", u=PACK),
+                ACT.Copy,
+                scale=g_cols[:, t : t + 1],
+            )
+
+        for pair in range(2):
+            for t in (2 * pair, 2 * pair + 1):
+                lift_gather_first(t)
+            for t in (2 * pair, 2 * pair + 1):
+                lift_gather_second(t)
+
+        wb_bf = [sb([P, HALF * PACK], BF16, "wb_bf%d" % h) for h in range(2)]
+        wb_codes = sb([P, N], U32, "wb_codes")
+        wb_scales = sb([P, N], U8, "wb_scales")
+        for h in range(2):
+            nc.scalar.copy(woven(wb_bf[h][:]), planes(wb_raw[:, :, cols(h)]))
+        lift_scatter_first(0)
+        lift_scatter_first(1)
+        for h in range(2):
+            quantise(wb_codes[:, cols(h)], wb_scales[:, cols(h)], wb_bf[h][:])
+        nc.vector.scalar_tensor_tensor(
+            gi_safe[:], g_cols[:, PACK : 2 * PACK], 0.0, g_cols[:, PACK : 2 * PACK], ALU.is_equal, ALU.add
+        )
+        lift_scatter_second(0)
+        nc.vector.reciprocal(gi_inv[:], gi_safe[:])
+        lift_scatter_second(1)
+
+        b_rows = [sb([P, N], F32, "b_rows%d" % t) for t in range(PACK)]
+        b_plain = sb([P, PACK, N], F32, "b_plain")
+        for t in range(PACK):
+            acc = bank(PACK + t)
+            tok = slice(t * P, (t + 1) * P)
+            product(acc[:], xb_words[:, tok], xb_scales[:, tok], wb_codes[:], wb_scales[:])
+            nc.scalar.activation(b_rows[t][:], acc[:], ACT.Copy, scale=gi_neg[:, t : t + 1])
+            nc.scalar.activation(b_plain[:, t, :], acc[:], ACT.Copy, scale=gi_neg[:, t : t + 1])
+
+        lift_scatter_first(2)
+        lift_scatter_first(3)
+
+        gap = [sb([P, PACK, HALF], F32, "gap%d" % h) for h in range(2)]
+        dist = [sb([P, PACK, HALF], F32, "dist%d" % h) for h in range(2)]
+        root = [sb([P, PACK, HALF], F32, "root%d" % h) for h in range(2)]
+        inv_den = [sb([P, PACK, HALF], F32, "inv_den%d" % h) for h in range(2)]
+        num = [sb([P, PACK, HALF], F32, "num%d" % h) for h in range(2)]
+        for h in range(2):
+            for t in range(PACK):
+                nc.vector.tensor_tensor(
+                    gap[h][:, t, :], b_rows[t][:].indirect(entries(n4_t, h)), b_plain[:, t, cols(h)], ALU.subtract
+                )
+                nc.scalar.activation(dist[h][:, t, :], gap[h][:, t, :], ACT.Abs, scale=gi_inv[:, t : t + 1])
+            nc.scalar.activation(root[h][:], dist[h][:], ACT.Abs_reciprocal_sqrt, bias=0.5)
+            nc.scalar.activation(inv_den[h][:], root[h][:], ACT.Square)
+
+        lift_scatter_second(2)
+        lift_scatter_second(3)
+
+        z_bf = sb([P, PACK, P * PACK], BF16, "z_bf")
+        z_codes = sb([P, H], U32, "z_codes")
+        z_scales = sb([P, H], U8, "z_scales")
+        for u in range(PACK):
+            nc.scalar.copy(woven(z_bf[:, u, :]), planes(z_dealt[:, :, u * P : (u + 1) * P]))
+
+        z2_bf = [sb([P, HALF * PACK], BF16, "z2_bf%d" % h) for h in range(2)]
+        z2_codes = sb([P, N], U32, "z2_codes")
+        z2_scales = sb([P, N], U8, "z2_scales")
+
+        def quantise_z(u):
+            feat = slice(u * P, (u + 1) * P)
+            quantise(z_codes[:, feat], z_scales[:, feat], z_bf[:, u, :])
+
+        for h in range(2):
+            for t in range(PACK):
+                nc.vector.tensor_tensor(
+                    num[h][:, t, :], b_rows[t][:].indirect(entries(n3_t, h)), b_plain[:, t, cols(h)], ALU.subtract
+                )
+            if h == 1:
+                quantise(z2_codes[:, cols(0)], z2_scales[:, cols(0)], z2_bf[0][:])
+            nc.vector.tensor_tensor(woven(z2_bf[h][:]), planes(num[h][:]), planes(inv_den[h][:]), ALU.mult)
+        quantise_z(0)
+        quantise(z2_codes[:, cols(1)], z2_scales[:, cols(1)], z2_bf[1][:])
+        for u in range(1, PACK):
+            quantise_z(u)
+
+        cv_rows = [sb([P, N], F32, "cv_rows%d" % u) for u in range(PACK)]
+        for u in range(PACK):
+            feat = slice(u * P, (u + 1) * P)
+            for h in range(2):
+                acc = bank(h * PACK + u)
+                product(acc[:, 0:HALF], z_codes[:, feat], z_scales[:, feat], z2_codes[:, cols(h)], z2_scales[:, cols(h)])
+                nc.scalar.activation(cv_rows[u][:, cols(h)], acc[:, 0:HALF], ACT.Copy, scale=0.0625)
+
+        at5 = [sb([P, PACK, HALF], F32, "at5_%d" % h) for h in range(2)]
+        at6 = [sb([P, PACK, HALF], F32, "at6_%d" % h) for h in range(2)]
+        larger = [sb([P, PACK, HALF], F32, "larger%d" % h) for h in range(2)]
+        result = [sb([P, PACK, HALF], F32, "result%d" % h) for h in range(2)]
+        out_bf = [sb([P, HALF * PACK], BF16, "out_bf%d" % h) for h in range(2)]
+        out_codes = sb([P, N], I32, "out_codes")
+        out_scales = sb([P, N], U8, "out_scales")
+        out_rows = out_0.rearrange("(p u) c -> p u c", u=PACK)
+        out_words = out_1[0].rearrange("p n t -> p (n t)").bitcast(I32)
+        for h in range(2):
+            for u in range(PACK):
+                nc.vector.tensor_copy(at5[h][:, u, :], cv_rows[u][:].indirect(entries(n5_t, h)))
+                nc.vector.tensor_copy(at6[h][:, u, :], cv_rows[u][:].indirect(entries(n6_t, h)))
+                nc.vector.tensor_tensor(larger[h][:, u, :], cv_rows[u][:, cols(h)], at5[h][:, u, :], ALU.max)
+            if h == 1:
+                quantise(out_codes[:, cols(0)], out_scales[:, cols(0)], out_bf[0][:])
+                nc.sync.dma_start(out_words[:, cols(0)], out_codes[:, cols(0)])
+            nc.vector.tensor_tensor(result[h][:], larger[h][:], at6[h][:], ALU.min)
+            nc.sync.dma_start(out_rows[:, :, cols(h)], result[h][:])
+            if h == 0:
+                nc.scalar.copy(woven(out_bf[h][:]), planes(result[h][:]))
+            else:
+                nc.vector.tensor_copy(woven(out_bf[h][:]), planes(result[h][:]))
+        quantise(out_codes[:, cols(1)], out_scales[:, cols(1)], out_bf[1][:])
+        nc.sync.dma_start(out_words[:, cols(1)], out_codes[:, cols(1)])
+        for q in range(4):
+            queue = nc.scalar if q % 2 == 0 else nc.sync
+            queue.dma_start(
+                out_2[0, 4 * q : 4 * q + 4, :].bitcast(I32), out_scales[32 * q : 32 * q + 4, :].bitcast(I32)
+            )

@@ -37,8 +37,8 @@ def tile_picked_mombliftfracminmx_none_po_kernel(
             nc.sync.dma_start(tile[:], src)
             return tile
 
-        def sb(shape, dtype, name):
-            return keep.tile(shape, dtype, name=name, align_bytes=64)
+        def sb(shape, dtype, name, tag=None):
+            return keep.tile(shape, dtype, name=name, tag=tag or name, align_bytes=64)
 
         def bank(j):
             return psum.tile([P, 512], F32, name="bank", tag="bank%d" % j)
@@ -49,11 +49,11 @@ def tile_picked_mombliftfracminmx_none_po_kernel(
         def entries(tile, h):
             return tile[:, h * HALF // PER_COL : (h + 1) * HALF // PER_COL]
 
-        def woven(ap):
-            return ap.rearrange("p (c i t) -> p c t i", i=RUN, t=PACK)
+        def woven(ap, run=RUN):
+            return ap.rearrange("p (c i t) -> p c t i", i=run, t=PACK)
 
-        def planes(ap):
-            return ap.rearrange("p t (c i) -> p c t i", i=RUN)
+        def planes(ap, run=RUN):
+            return ap.rearrange("p t (c i) -> p c t i", i=run)
 
         offs_t = load_list(offs, "offs_t")
         xw = sb([P, T], I32, "xw")
@@ -75,6 +75,8 @@ def tile_picked_mombliftfracminmx_none_po_kernel(
         nc.gpsimd.memset(g_rows[:], 0.0)
         ident = sb([P, P], F32, "ident")
         make_identity(nc, ident[:])
+        warm = sb([P, 1], F32, "warm")
+        nc.scalar.activation(warm[:], g_rows[:, 0:1], ACT.Abs_reciprocal_sqrt, bias=0.5)
         for j, g in enumerate((gt, gi)):
             nc.sync.dma_start(
                 g_rows[PACK * j : PACK * (j + 1), :].rearrange("t (c b) -> t c b", b=4),
@@ -92,8 +94,8 @@ def tile_picked_mombliftfracminmx_none_po_kernel(
             )
             return words
 
-        def pick_scales(lst, name):
-            raw = sb([P, S], U8, name + "_raw")
+        def pick_scales(lst, name, tag=None):
+            raw = sb([P, S], U8, name + "_raw", tag)
             nc.vector.tensor_copy(raw[:], xs[:].indirect(lst[:]))
             dealt = sb([P, S], U8, name)
             nc.vector.tensor_copy(
@@ -126,7 +128,7 @@ def tile_picked_mombliftfracminmx_none_po_kernel(
         for h in range(2):
             nc.scalar.copy(woven(wa_bf[h][:]), planes(wa_raw[h][:]))
             quantise(wa_codes[:, cols(h)], wa_scales[:, cols(h)], wa_bf[h][:])
-        xb_scales = pick_scales(two_t, "xb_scales")
+        xb_scales = pick_scales(two_t, "xb_scales", "wa_bf1")
 
         a_rows = [sb([P, H], F32, "a_rows%d" % t) for t in range(PACK)]
         for t in range(PACK):
@@ -134,6 +136,12 @@ def tile_picked_mombliftfracminmx_none_po_kernel(
             tok = slice(t * P, (t + 1) * P)
             product(acc[:], xa_words[:, tok], xa_scales[:, tok], wa_codes[:], wa_scales[:])
             nc.scalar.copy(a_rows[t][:], acc[:])
+
+        wb_bf = [sb([P, HALF * PACK], BF16, "wb_bf%d" % h) for h in range(2)]
+        wb_codes = sb([P, N], U32, "wb_codes")
+        wb_scales = sb([P, N], U8, "wb_scales")
+        for h in range(2):
+            nc.scalar.copy(woven(wb_bf[h][:]), planes(wb_raw[:, :, cols(h)]))
 
         g_ps = bank(PACK)
         nc.tensor.transpose(g_ps[:, 0:P], g_rows[:], ident[:])
@@ -148,7 +156,7 @@ def tile_picked_mombliftfracminmx_none_po_kernel(
         pos_half = [sb([P, W], F32, "pos_half%d" % t) for t in range(PACK)]
         excess = [sb([P, W], F32, "excess%d" % t) for t in range(PACK)]
         over = [sb([P, W], F32, "over%d" % t) for t in range(PACK)]
-        dt = [sb([P, H], F32, "dt%d" % t) for t in range(PACK)]
+        dt = {}
         z_dealt = sb([P, PACK, H], F32, "z_dealt")
 
         def lift_gather_first(t):
@@ -159,11 +167,14 @@ def tile_picked_mombliftfracminmx_none_po_kernel(
             nc.vector.tensor_tensor(excess[t][:], a_rows[t][:].indirect(n2_t[:]), neg_half[t][:], ALU.add)
             nc.scalar.activation(over[t][:], excess[t][:], ACT.Relu)
 
-        def lift_scatter_first(t):
+        def lift_scatter_first(t, tag=None):
+            dt[t] = sb([P, H], F32, "dt%d" % t, tag)
             nc.vector.tensor_tensor(dt[t][:].indirect(n1_t[:]), excess[t][:], neg_half[t][:], ALU.add)
 
         def lift_scatter_second(t):
             nc.vector.tensor_tensor(dt[t][:].indirect(n2_t[:]), over[t][:], pos_half[t][:], ALU.add)
+
+        def weigh_z(t):
             nc.scalar.activation(
                 z_dealt[:, t, :].rearrange("p (u m) -> p m u", u=PACK),
                 dt[t][:].rearrange("p (m u) -> p m u", u=PACK),
@@ -177,15 +188,10 @@ def tile_picked_mombliftfracminmx_none_po_kernel(
             for t in (2 * pair, 2 * pair + 1):
                 lift_gather_second(t)
 
-        wb_bf = [sb([P, HALF * PACK], BF16, "wb_bf%d" % h) for h in range(2)]
-        wb_codes = sb([P, N], U32, "wb_codes")
-        wb_scales = sb([P, N], U8, "wb_scales")
-        for h in range(2):
-            nc.scalar.copy(woven(wb_bf[h][:]), planes(wb_raw[:, :, cols(h)]))
         lift_scatter_first(0)
-        lift_scatter_first(1)
         for h in range(2):
             quantise(wb_codes[:, cols(h)], wb_scales[:, cols(h)], wb_bf[h][:])
+        lift_scatter_first(1, "wb_bf1")
         nc.vector.scalar_tensor_tensor(
             gi_safe[:], g_cols[:, PACK : 2 * PACK], 0.0, g_cols[:, PACK : 2 * PACK], ALU.is_equal, ALU.add
         )
@@ -202,25 +208,32 @@ def tile_picked_mombliftfracminmx_none_po_kernel(
             nc.scalar.activation(b_rows[t][:], acc[:], ACT.Copy, scale=gi_neg[:, t : t + 1])
             nc.scalar.activation(b_plain[:, t, :], acc[:], ACT.Copy, scale=gi_neg[:, t : t + 1])
 
-        lift_scatter_first(2)
-        lift_scatter_first(3)
+        weigh_z(0)
+        weigh_z(1)
 
-        gap = [sb([P, PACK, HALF], F32, "gap%d" % h) for h in range(2)]
-        dist = [sb([P, PACK, HALF], F32, "dist%d" % h) for h in range(2)]
-        root = [sb([P, PACK, HALF], F32, "root%d" % h) for h in range(2)]
-        inv_den = [sb([P, PACK, HALF], F32, "inv_den%d" % h) for h in range(2)]
-        num = [sb([P, PACK, HALF], F32, "num%d" % h) for h in range(2)]
-        for h in range(2):
-            for t in range(PACK):
+        gap = [sb([P, N], F32, "gap%d" % t) for t in range(PACK)]
+        dist = sb([P, PACK, N], F32, "dist")
+        root = sb([P, PACK, N], F32, "root")
+        inv_den = sb([P, PACK, N], F32, "inv_den")
+        num = sb([P, PACK, N], F32, "num")
+        for t in range(PACK):
+            for h in range(2):
                 nc.vector.tensor_tensor(
-                    gap[h][:, t, :], b_rows[t][:].indirect(entries(n4_t, h)), b_plain[:, t, cols(h)], ALU.subtract
+                    gap[t][:, cols(h)], b_rows[t][:].indirect(entries(n4_t, h)), b_plain[:, t, cols(h)], ALU.subtract
                 )
-                nc.scalar.activation(dist[h][:, t, :], gap[h][:, t, :], ACT.Abs, scale=gi_inv[:, t : t + 1])
-            nc.scalar.activation(root[h][:], dist[h][:], ACT.Abs_reciprocal_sqrt, bias=0.5)
-            nc.scalar.activation(inv_den[h][:], root[h][:], ACT.Square)
+            nc.scalar.activation(dist[:, t, :], gap[t][:], ACT.Abs, scale=gi_inv[:, t : t + 1])
+            nc.scalar.activation(root[:, t, :], dist[:, t, :], ACT.Abs_reciprocal_sqrt, bias=0.5)
+            nc.scalar.activation(inv_den[:, t, :], root[:, t, :], ACT.Square)
+            for h in range(2):
+                nc.vector.tensor_tensor(
+                    num[:, t, cols(h)], b_rows[t][:].indirect(entries(n3_t, h)), b_plain[:, t, cols(h)], ALU.subtract
+                )
 
-        lift_scatter_second(2)
-        lift_scatter_second(3)
+        lift_scatter_first(2, "gap2")
+        lift_scatter_first(3, "gap3")
+        for t in (2, 3):
+            lift_scatter_second(t)
+            weigh_z(t)
 
         z_bf = sb([P, PACK, P * PACK], BF16, "z_bf")
         z_codes = sb([P, H], U32, "z_codes")
@@ -231,31 +244,22 @@ def tile_picked_mombliftfracminmx_none_po_kernel(
         z2_bf = [sb([P, HALF * PACK], BF16, "z2_bf%d" % h) for h in range(2)]
         z2_codes = sb([P, N], U32, "z2_codes")
         z2_scales = sb([P, N], U8, "z2_scales")
-
-        def quantise_z(u):
+        for h in range(2):
+            nc.vector.tensor_tensor(
+                woven(z2_bf[h][:], 2), planes(num[:, :, cols(h)], 2), planes(inv_den[:, :, cols(h)], 2), ALU.mult
+            )
+        for h in range(2):
+            quantise(z2_codes[:, cols(h)], z2_scales[:, cols(h)], z2_bf[h][:])
+        for u in range(PACK):
             feat = slice(u * P, (u + 1) * P)
             quantise(z_codes[:, feat], z_scales[:, feat], z_bf[:, u, :])
-
-        for h in range(2):
-            for t in range(PACK):
-                nc.vector.tensor_tensor(
-                    num[h][:, t, :], b_rows[t][:].indirect(entries(n3_t, h)), b_plain[:, t, cols(h)], ALU.subtract
-                )
-            if h == 1:
-                quantise(z2_codes[:, cols(0)], z2_scales[:, cols(0)], z2_bf[0][:])
-            nc.vector.tensor_tensor(woven(z2_bf[h][:]), planes(num[h][:]), planes(inv_den[h][:]), ALU.mult)
-        quantise_z(0)
-        quantise(z2_codes[:, cols(1)], z2_scales[:, cols(1)], z2_bf[1][:])
-        for u in range(1, PACK):
-            quantise_z(u)
 
         cv_rows = [sb([P, N], F32, "cv_rows%d" % u) for u in range(PACK)]
         for u in range(PACK):
             feat = slice(u * P, (u + 1) * P)
-            for h in range(2):
-                acc = bank(h * PACK + u)
-                product(acc[:, 0:HALF], z_codes[:, feat], z_scales[:, feat], z2_codes[:, cols(h)], z2_scales[:, cols(h)])
-                nc.scalar.activation(cv_rows[u][:, cols(h)], acc[:, 0:HALF], ACT.Copy, scale=0.0625)
+            acc = bank(u)
+            product(acc[:], z_codes[:, feat], z_scales[:, feat], z2_codes[:], z2_scales[:])
+            nc.scalar.activation(cv_rows[u][:], acc[:], ACT.Copy, scale=0.0625)
 
         at5 = [sb([P, PACK, HALF], F32, "at5_%d" % h) for h in range(2)]
         at6 = [sb([P, PACK, HALF], F32, "at6_%d" % h) for h in range(2)]

@@ -46,18 +46,15 @@ def tile_picked_mombliftfracminmx_none_po_kernel(
         def cols(h):
             return slice(h * HALF, (h + 1) * HALF)
 
-        def entries(tile, h):
-            return tile[:, h * HALF // PER_COL : (h + 1) * HALF // PER_COL]
-
         def woven(ap, run=RUN):
             return ap.rearrange("p (c i t) -> p c t i", i=run, t=PACK)
 
         def planes(ap, run=RUN):
             return ap.rearrange("p t (c i) -> p c t i", i=run)
 
-        offs_t = load_list(offs, "offs_t")
         xw = sb([P, T], I32, "xw")
         nc.sync.dma_start(xw[:], x_words[0].rearrange("p n t -> p (n t)").bitcast(I32))
+        offs_t = load_list(offs, "offs_t")
         xs = sb([P, T], U8, "xs")
         nc.vector.memset(xs[:].bitcast(I32), 0)
         for q in range(4):
@@ -199,14 +196,14 @@ def tile_picked_mombliftfracminmx_none_po_kernel(
         nc.vector.reciprocal(gi_inv[:], gi_safe[:])
         lift_scatter_second(1)
 
-        b_rows = [sb([P, N], F32, "b_rows%d" % t) for t in range(PACK)]
-        b_plain = sb([P, PACK, N], F32, "b_plain")
+        rows = [sb([P, 2 * N], F32, "rows%d" % t) for t in range(PACK)]
+        b_plain = [rows[t ^ 1][:, N : 2 * N] for t in range(PACK)]
         for t in range(PACK):
             acc = bank(PACK + t)
             tok = slice(t * P, (t + 1) * P)
             product(acc[:], xb_words[:, tok], xb_scales[:, tok], wb_codes[:], wb_scales[:])
-            nc.scalar.activation(b_rows[t][:], acc[:], ACT.Copy, scale=gi_neg[:, t : t + 1])
-            nc.scalar.activation(b_plain[:, t, :], acc[:], ACT.Copy, scale=gi_neg[:, t : t + 1])
+            nc.scalar.activation(rows[t][:, 0:N], acc[:], ACT.Copy, scale=gi_neg[:, t : t + 1])
+            nc.scalar.activation(b_plain[t], acc[:], ACT.Copy, scale=gi_neg[:, t : t + 1])
 
         weigh_z(0)
         weigh_z(1)
@@ -217,17 +214,11 @@ def tile_picked_mombliftfracminmx_none_po_kernel(
         inv_den = sb([P, PACK, N], F32, "inv_den")
         num = sb([P, PACK, N], F32, "num")
         for t in range(PACK):
-            for h in range(2):
-                nc.vector.tensor_tensor(
-                    gap[t][:, cols(h)], b_rows[t][:].indirect(entries(n4_t, h)), b_plain[:, t, cols(h)], ALU.subtract
-                )
+            nc.vector.tensor_tensor(gap[t][:], rows[t][:].indirect(n4_t[:]), b_plain[t], ALU.subtract)
             nc.scalar.activation(dist[:, t, :], gap[t][:], ACT.Abs, scale=gi_inv[:, t : t + 1])
             nc.scalar.activation(root[:, t, :], dist[:, t, :], ACT.Abs_reciprocal_sqrt, bias=0.5)
             nc.scalar.activation(inv_den[:, t, :], root[:, t, :], ACT.Square)
-            for h in range(2):
-                nc.vector.tensor_tensor(
-                    num[:, t, cols(h)], b_rows[t][:].indirect(entries(n3_t, h)), b_plain[:, t, cols(h)], ALU.subtract
-                )
+            nc.vector.tensor_tensor(num[:, t, :], rows[t][:].indirect(n3_t[:]), b_plain[t], ALU.subtract)
 
         lift_scatter_first(2, "gap2")
         lift_scatter_first(3, "gap3")
@@ -235,57 +226,68 @@ def tile_picked_mombliftfracminmx_none_po_kernel(
             lift_scatter_second(t)
             weigh_z(t)
 
-        z_bf = sb([P, PACK, P * PACK], BF16, "z_bf")
+        z_bf = [sb([P, P * PACK], BF16, "z_bf%d" % u) for u in range(PACK)]
         z_codes = sb([P, H], U32, "z_codes")
         z_scales = sb([P, H], U8, "z_scales")
         for u in range(PACK):
-            nc.scalar.copy(woven(z_bf[:, u, :]), planes(z_dealt[:, :, u * P : (u + 1) * P]))
+            nc.scalar.copy(woven(z_bf[u][:]), planes(z_dealt[:, :, u * P : (u + 1) * P]))
 
         z2_bf = [sb([P, HALF * PACK], BF16, "z2_bf%d" % h) for h in range(2)]
-        z2_codes = sb([P, N], U32, "z2_codes")
-        z2_scales = sb([P, N], U8, "z2_scales")
         for h in range(2):
             nc.vector.tensor_tensor(
                 woven(z2_bf[h][:], 2), planes(num[:, :, cols(h)], 2), planes(inv_den[:, :, cols(h)], 2), ALU.mult
             )
-        for h in range(2):
-            quantise(z2_codes[:, cols(h)], z2_scales[:, cols(h)], z2_bf[h][:])
+        z2_scales = sb([P, N], U8, "z2_scales")
+
+        def quantise_z(u):
+            feat = slice(u * P, (u + 1) * P)
+            quantise(z_codes[:, feat], z_scales[:, feat], z_bf[u][:])
+
+        z2_codes = [sb([P, HALF], U32, "z2_codes0")]
+        quantise(z2_codes[0][:], z2_scales[:, cols(0)], z2_bf[0][:])
+        quantise_z(0)
+        z2_codes.append(sb([P, HALF], U32, "z2_codes1", "z_bf0"))
+        quantise(z2_codes[1][:], z2_scales[:, cols(1)], z2_bf[1][:])
+        for u in range(1, PACK):
+            quantise_z(u)
+
         for u in range(PACK):
             feat = slice(u * P, (u + 1) * P)
-            quantise(z_codes[:, feat], z_scales[:, feat], z_bf[:, u, :])
+            for h in range(2):
+                acc = bank(h * PACK + u)
+                product(acc[:, 0:HALF], z_codes[:, feat], z_scales[:, feat], z2_codes[h][:], z2_scales[:, cols(h)])
+                nc.scalar.activation(rows[u][:, cols(h)], acc[:, 0:HALF], ACT.Copy, scale=0.0625)
 
-        cv_rows = [sb([P, N], F32, "cv_rows%d" % u) for u in range(PACK)]
-        for u in range(PACK):
-            feat = slice(u * P, (u + 1) * P)
-            acc = bank(u)
-            product(acc[:], z_codes[:, feat], z_scales[:, feat], z2_codes[:], z2_scales[:])
-            nc.scalar.activation(cv_rows[u][:], acc[:], ACT.Copy, scale=0.0625)
-
-        at5 = [sb([P, PACK, HALF], F32, "at5_%d" % h) for h in range(2)]
-        at6 = [sb([P, PACK, HALF], F32, "at6_%d" % h) for h in range(2)]
-        larger = [sb([P, PACK, HALF], F32, "larger%d" % h) for h in range(2)]
-        result = [sb([P, PACK, HALF], F32, "result%d" % h) for h in range(2)]
+        at5 = sb([P, PACK, N], F32, "at5")
+        at6 = sb([P, PACK, N], F32, "at6")
+        larger = sb([P, PACK, N], F32, "larger")
+        result = sb([P, PACK, N], F32, "result")
         out_bf = [sb([P, HALF * PACK], BF16, "out_bf%d" % h) for h in range(2)]
         out_codes = sb([P, N], I32, "out_codes")
         out_scales = sb([P, N], U8, "out_scales")
         out_rows = out_0.rearrange("(p u) c -> p u c", u=PACK)
         out_words = out_1[0].rearrange("p n t -> p (n t)").bitcast(I32)
+
+        def fetch(dst, lst, u, span):
+            nc.vector.tensor_copy(dst[:, u, span], rows[u][:].indirect(lst[:, span.start // PER_COL : span.stop // PER_COL]))
+
+        def finish(u, span):
+            nc.vector.tensor_tensor(result[:, u, span], larger[:, u, span], at6[:, u, span], ALU.min)
+            nc.sync.dma_start(out_rows[:, u, span], result[:, u, span])
+
+        pieces = [(u, slice(0, N)) for u in range(PACK - 1)] + [(PACK - 1, cols(h)) for h in range(2)]
+        for j, (u, span) in enumerate(pieces):
+            fetch(at5, n5_t, u, span)
+            if j > 0:
+                finish(*pieces[j - 1])
+            fetch(at6, n6_t, u, span)
+            nc.vector.tensor_tensor(larger[:, u, span], rows[u][:, span], at5[:, u, span], ALU.max)
+        nc.scalar.copy(woven(out_bf[0][:]), planes(result[:, :, cols(0)]))
+        finish(*pieces[-1])
+        nc.vector.tensor_copy(woven(out_bf[1][:]), planes(result[:, :, cols(1)]))
         for h in range(2):
-            for u in range(PACK):
-                nc.vector.tensor_copy(at5[h][:, u, :], cv_rows[u][:].indirect(entries(n5_t, h)))
-                nc.vector.tensor_copy(at6[h][:, u, :], cv_rows[u][:].indirect(entries(n6_t, h)))
-                nc.vector.tensor_tensor(larger[h][:, u, :], cv_rows[u][:, cols(h)], at5[h][:, u, :], ALU.max)
-            if h == 1:
-                quantise(out_codes[:, cols(0)], out_scales[:, cols(0)], out_bf[0][:])
-                nc.sync.dma_start(out_words[:, cols(0)], out_codes[:, cols(0)])
-            nc.vector.tensor_tensor(result[h][:], larger[h][:], at6[h][:], ALU.min)
-            nc.sync.dma_start(out_rows[:, :, cols(h)], result[h][:])
-            if h == 0:
-                nc.scalar.copy(woven(out_bf[h][:]), planes(result[h][:]))
-            else:
-                nc.vector.tensor_copy(woven(out_bf[h][:]), planes(result[h][:]))
-        quantise(out_codes[:, cols(1)], out_scales[:, cols(1)], out_bf[1][:])
-        nc.sync.dma_start(out_words[:, cols(1)], out_codes[:, cols(1)])
+            quantise(out_codes[:, cols(h)], out_scales[:, cols(h)], out_bf[h][:])
+            nc.sync.dma_start(out_words[:, cols(h)], out_codes[:, cols(h)])
         for q in range(4):
             queue = nc.scalar if q % 2 == 0 else nc.sync
             queue.dma_start(

@@ -129,25 +129,12 @@ def tile_picked_mombliftfracminmx_none_po_kernel(
 
         a_rows = [sb([P, H], F32, "a_rows%d" % t) for t in range(PACK)]
         for t in range(PACK):
-            acc = bank(t)
             tok = slice(t * P, (t + 1) * P)
-            product(acc[:], xa_words[:, tok], xa_scales[:, tok], wa_codes[:], wa_scales[:])
-            nc.scalar.copy(a_rows[t][:], acc[:])
-
-        wb_bf = [sb([P, HALF * PACK], BF16, "wb_bf%d" % h) for h in range(2)]
-        wb_codes = sb([P, N], U32, "wb_codes")
-        wb_scales = sb([P, N], U8, "wb_scales")
-        for h in range(2):
-            nc.scalar.copy(woven(wb_bf[h][:]), planes(wb_raw[:, :, cols(h)]))
-
-        g_ps = bank(PACK)
-        nc.tensor.transpose(g_ps[:, 0:P], g_rows[:], ident[:])
-        g_cols = sb([P, 2 * PACK], F32, "g_cols")
-        nc.scalar.copy(g_cols[:], g_ps[:, 0 : 2 * PACK])
-        gi_neg = sb([P, PACK], F32, "gi_neg")
-        nc.scalar.activation(gi_neg[:], g_ps[:, PACK : 2 * PACK], ACT.Copy, scale=-1.0)
-        gi_safe = sb([P, PACK], F32, "gi_safe")
-        gi_inv = sb([P, PACK], F32, "gi_inv")
+            spans = [cols(0), cols(1)] if t == 0 else [slice(0, H)]
+            for j, span in enumerate(spans):
+                acc = bank(t + PACK * j)
+                product(acc[:, span], xa_words[:, tok], xa_scales[:, tok], wa_codes[:, span], wa_scales[:, span])
+                nc.scalar.copy(a_rows[t][:, span], acc[:, span])
 
         neg_half = [sb([P, W], F32, "neg_half%d" % t) for t in range(PACK)]
         pos_half = [sb([P, W], F32, "pos_half%d" % t) for t in range(PACK)]
@@ -161,7 +148,7 @@ def tile_picked_mombliftfracminmx_none_po_kernel(
             nc.scalar.activation(pos_half[t][:], neg_half[t][:], ACT.Copy, scale=-1.0)
 
         def lift_gather_second(t):
-            nc.vector.tensor_tensor(excess[t][:], a_rows[t][:].indirect(n2_t[:]), neg_half[t][:], ALU.add)
+            nc.vector.tensor_tensor(excess[t][:], a_rows[t][:].indirect(n2_t[:]), pos_half[t][:], ALU.subtract)
             nc.scalar.activation(over[t][:], excess[t][:], ACT.Relu)
 
         def lift_scatter_first(t, tag=None):
@@ -179,20 +166,35 @@ def tile_picked_mombliftfracminmx_none_po_kernel(
                 scale=g_cols[:, t : t + 1],
             )
 
-        for pair in range(2):
-            for t in (2 * pair, 2 * pair + 1):
-                lift_gather_first(t)
-            for t in (2 * pair, 2 * pair + 1):
-                lift_gather_second(t)
+        for t in range(PACK):
+            lift_gather_first(t)
+
+        wb_bf = [sb([P, HALF * PACK], BF16, "wb_bf%d" % h) for h in range(2)]
+        wb_codes = sb([P, N], U32, "wb_codes")
+        wb_scales = sb([P, N], U8, "wb_scales")
+        for h in range(2):
+            nc.scalar.copy(woven(wb_bf[h][:]), planes(wb_raw[:, :, cols(h)]))
+
+        g_ps = bank(PACK)
+        nc.tensor.transpose(g_ps[:, 0:P], g_rows[:], ident[:])
+        g_cols = sb([P, 2 * PACK], F32, "g_cols")
+        nc.scalar.copy(g_cols[:], g_ps[:, 0 : 2 * PACK])
+        gi_neg = sb([P, PACK], F32, "gi_neg")
+        nc.scalar.activation(gi_neg[:], g_ps[:, PACK : 2 * PACK], ACT.Copy, scale=-1.0)
+        gi_safe = sb([P, PACK], F32, "gi_safe")
+        gi_inv = sb([P, PACK], F32, "gi_inv")
+
+        for t in range(PACK):
+            lift_gather_second(t)
 
         lift_scatter_first(0)
         for h in range(2):
             quantise(wb_codes[:, cols(h)], wb_scales[:, cols(h)], wb_bf[h][:])
-        lift_scatter_first(1, "wb_bf1")
         nc.vector.scalar_tensor_tensor(
             gi_safe[:], g_cols[:, PACK : 2 * PACK], 0.0, g_cols[:, PACK : 2 * PACK], ALU.is_equal, ALU.add
         )
         lift_scatter_second(0)
+        lift_scatter_first(1, "wb_bf1")
         nc.vector.reciprocal(gi_inv[:], gi_safe[:])
         lift_scatter_second(1)
 
@@ -251,10 +253,12 @@ def tile_picked_mombliftfracminmx_none_po_kernel(
         for u in range(1, PACK):
             quantise_z(u)
 
+        sums = {}
         for u in range(PACK):
             feat = slice(u * P, (u + 1) * P)
             for h in range(2):
                 acc = bank(h * PACK + u)
+                sums[u, h] = acc
                 product(acc[:, 0:HALF], z_codes[:, feat], z_scales[:, feat], z2_codes[h][:], z2_scales[:, cols(h)])
                 nc.scalar.activation(rows[u][:, cols(h)], acc[:, 0:HALF], ACT.Copy, scale=0.0625)
 
@@ -271,19 +275,42 @@ def tile_picked_mombliftfracminmx_none_po_kernel(
         def fetch(dst, lst, u, span):
             nc.vector.tensor_copy(dst[:, u, span], rows[u][:].indirect(lst[:, span.start // PER_COL : span.stop // PER_COL]))
 
+        def take_larger(u, h):
+            nc.vector.scalar_tensor_tensor(
+                larger[:, u, cols(h)], sums[u, h][:, 0:HALF], 0.0625, at5[:, u, cols(h)], ALU.mult, ALU.max
+            )
+
         def finish(u, span):
             nc.vector.tensor_tensor(result[:, u, span], larger[:, u, span], at6[:, u, span], ALU.min)
             nc.sync.dma_start(out_rows[:, u, span], result[:, u, span])
 
-        pieces = [(u, slice(0, N)) for u in range(PACK - 1)] + [(PACK - 1, cols(h)) for h in range(2)]
-        for j, (u, span) in enumerate(pieces):
-            fetch(at5, n5_t, u, span)
-            if j > 0:
-                finish(*pieces[j - 1])
-            fetch(at6, n6_t, u, span)
-            nc.vector.tensor_tensor(larger[:, u, span], rows[u][:, span], at5[:, u, span], ALU.max)
+        def finish_aside(u):
+            above = sb([P, N], F32, "above%d" % u)
+            cut = sb([P, N], F32, "cut%d" % u)
+            nc.gpsimd.tensor_tensor(above[:], larger[:, u, :], at6[:, u, :], ALU.subtract)
+            nc.scalar.activation(cut[:], above[:], ACT.Relu)
+            nc.gpsimd.tensor_tensor(result[:, u, :], larger[:, u, :], cut[:], ALU.subtract)
+            nc.sync.dma_start(out_rows[:, u, :], result[:, u, :])
+
+        whole = slice(0, N)
+        for u in range(PACK - 1):
+            fetch(at5, n5_t, u, whole)
+            fetch(at6, n6_t, u, whole)
+            for h in range(2):
+                take_larger(u, h)
+            if u < 2:
+                finish_aside(u)
+        last = PACK - 1
+        fetch(at5, n5_t, last, cols(0))
+        fetch(at6, n6_t, last, cols(0))
+        take_larger(last, 0)
+        finish(last - 1, whole)
+        fetch(at5, n5_t, last, cols(1))
+        finish(last, cols(0))
+        fetch(at6, n6_t, last, cols(1))
+        take_larger(last, 1)
         nc.scalar.copy(woven(out_bf[0][:]), planes(result[:, :, cols(0)]))
-        finish(*pieces[-1])
+        finish(last, cols(1))
         nc.vector.tensor_copy(woven(out_bf[1][:]), planes(result[:, :, cols(1)]))
         for h in range(2):
             quantise(out_codes[:, cols(h)], out_scales[:, cols(h)], out_bf[h][:])

from contextlib import ExitStack

import concourse.mybir as mybir
from concourse.masks import make_identity

K, T, S, N, H, W = 512, 2048, 512, 512, 512, 256
FLOPS = 2 * K * S * H + 2 * K * S * N + 2 * S * H * N

F32 = mybir.dt.float32
BF16 = mybir.dt.bfloat16
I32 = mybir.dt.int32
U32 = mybir.dt.uint32
U16 = mybir.dt.uint16
U8 = mybir.dt.uint8
FP8X4 = mybir.dt.float8_e4m3fn_x4
ALU = mybir.AluOpType
ACT = mybir.ActivationFunctionType

P = 128
PACK = 4
HALF = 256
RUN = 4
PER_COL = 16


def tile_picked_mombliftfracminmx_none_po_kernel(
    tc, x_words, x_scales, wa, wb, gt, gi, offs, two, n1, n2, n3, n4, n5, n6, out_0, out_1, out_2
):
    nc = tc.nc
    with ExitStack() as ctx:
        held = ctx.enter_context(tc.tile_pool(name="held", bufs=1))
        keep = ctx.enter_context(tc.tile_pool(name="keep", bufs=1))
        psum = ctx.enter_context(tc.psum_pool(name="psum", bufs=1))

        def load_list(src, name):
            tile = held.tile(list(src.shape), U16, name=name)
            nc.sync.dma_start(tile[:], src)
            return tile

        def sb(shape, dtype, name, tag=None):
            return keep.tile(shape, dtype, name=name, tag=tag or name, align_bytes=64)

        def bank(j):
            return psum.tile([P, 512], F32, name="bank", tag="bank%d" % j)

        def cols(h):
            return slice(h * HALF, (h + 1) * HALF)

        def woven(ap, run=RUN):
            return ap.rearrange("p (c i t) -> p c t i", i=run, t=PACK)

        def planes(ap, run=RUN):
            return ap.rearrange("p t (c i) -> p c t i", i=run)

        xw = sb([P, T], I32, "xw")
        nc.sync.dma_start(xw[:], x_words[0].rearrange("p n t -> p (n t)").bitcast(I32))
        offs_t = load_list(offs, "offs_t")
        xs = sb([P, T], U8, "xs")
        nc.vector.memset(xs[:].bitcast(I32), 0)
        for q in range(4):
            nc.scalar.dma_start(xs[32 * q : 32 * q + 4, :].bitcast(I32), x_scales[0, 4 * q : 4 * q + 4, :].bitcast(I32))
        two_t = load_list(two, "two_t")
        wa_rows = wa.rearrange("(p j) c -> p j c", j=PACK)
        wa_raw = [sb([P, PACK, HALF], F32, "wa_raw%d" % h) for h in range(2)]
        for h in range(2):
            nc.sync.dma_start(wa_raw[h][:], wa_rows[:, :, cols(h)])
        n1_t = load_list(n1, "n1_t")
        n2_t = load_list(n2, "n2_t")
        wb_raw = sb([P, PACK, N], F32, "wb_raw")
        nc.sync.dma_start(wb_raw[:], wb.rearrange("(p j) c -> p j c", j=PACK))
        g_rows = sb([P, P], F32, "g_rows")
        nc.gpsimd.memset(g_rows[:], 0.0)
        ident = sb([P, P], F32, "ident")
        make_identity(nc, ident[:])
        warm = sb([P, 1], F32, "warm")
        nc.scalar.activation(warm[:], g_rows[:, 0:1], ACT.Abs_reciprocal_sqrt, bias=0.5)
        for j, g in enumerate((gt, gi)):
            nc.sync.dma_start(
                g_rows[PACK * j : PACK * (j + 1), :].rearrange("t (c b) -> t c b", b=4),
                g.rearrange("(c t b) o -> t c (b o)", t=PACK, b=4),
            )
        n4_t = load_list(n4, "n4_t")
        n3_t = load_list(n3, "n3_t")
        n5_t = load_list(n5, "n5_t")
        n6_t = load_list(n6, "n6_t")

        def pick_words(lst, name):
            words = sb([P, S], U32, name)
            nc.vector.tensor_copy(
                words[:].rearrange("p (t c b) -> p c t b", t=PACK, b=4), xw[:].bitcast(U32).indirect(lst[:])
            )
            return words

        def pick_scales(lst, name, tag=None):
            raw = sb([P, S], U8, name + "_raw", tag)
            nc.vector.tensor_copy(raw[:], xs[:].indirect(lst[:]))
            dealt = sb([P, S], U8, name)
            nc.vector.tensor_copy(
                dealt[:].bitcast(I32).rearrange("p (t c) -> p t c", t=PACK),
                raw[:].bitcast(I32).rearrange("p (c t) -> p t c", t=PACK),
            )
            return dealt

        def quantise(codes, scales, grouped):
            nc.vector.quantize_mx(out=codes.bitcast(FP8X4), scales=scales, in_=grouped)

        def product(out, lhs_codes, lhs_scales, rhs_codes, rhs_scales):
            nc.tensor.matmul_mx(
                out=out,
                lhsT=lhs_codes.bitcast(FP8X4),
                lhsT_scale=lhs_scales,
                rhs=rhs_codes.bitcast(FP8X4),
                rhs_scale=rhs_scales,
                start=True,
                stop=True,
            )

        xa_words = pick_words(offs_t, "xa_words")
        xb_words = pick_words(two_t, "xb_words")
        xa_scales = pick_scales(offs_t, "xa_scales")

        wa_bf = [sb([P, HALF * PACK], BF16, "wa_bf%d" % h) for h in range(2)]
        wa_codes = sb([P, H], U32, "wa_codes")
        wa_scales = sb([P, H], U8, "wa_scales")
        for h in range(2):
            nc.scalar.copy(woven(wa_bf[h][:]), planes(wa_raw[h][:]))
            quantise(wa_codes[:, cols(h)], wa_scales[:, cols(h)], wa_bf[h][:])
        xb_scales = pick_scales(two_t, "xb_scales", "wa_bf1")

        a_rows = [sb([P, H], F32, "a_rows%d" % t) for t in range(PACK)]
        for t in range(PACK):
            tok = slice(t * P, (t + 1) * P)
            spans = [cols(0), cols(1)] if t == 0 else [slice(0, H)]
            for j, span in enumerate(spans):
                acc = bank(t + PACK * j)
                product(acc[:, span], xa_words[:, tok], xa_scales[:, tok], wa_codes[:, span], wa_scales[:, span])
                nc.scalar.copy(a_rows[t][:, span], acc[:, span])

        neg_half = [sb([P, W], F32, "neg_half%d" % t) for t in range(PACK)]
        pos_half = [sb([P, W], F32, "pos_half%d" % t) for t in range(PACK)]
        excess = [sb([P, W], F32, "excess%d" % t) for t in range(PACK)]
        over = [sb([P, W], F32, "over%d" % t) for t in range(PACK)]
        dt = {}
        z_dealt = sb([P, PACK, H], F32, "z_dealt")

        def lift_gather_first(t):
            nc.vector.tensor_scalar(neg_half[t][:], a_rows[t][:].indirect(n1_t[:]), -0.5, 0.0, ALU.mult, ALU.add)
            nc.scalar.activation(pos_half[t][:], neg_half[t][:], ACT.Copy, scale=-1.0)

        def lift_gather_second(t):
            nc.vector.tensor_tensor(excess[t][:], a_rows[t][:].indirect(n2_t[:]), pos_half[t][:], ALU.subtract)
            nc.scalar.activation(over[t][:], excess[t][:], ACT.Relu)

        def lift_scatter_first(t, tag=None):
            dt[t] = sb([P, H], F32, "dt%d" % t, tag)
            nc.vector.tensor_tensor(dt[t][:].indirect(n1_t[:]), excess[t][:], neg_half[t][:], ALU.add)

        def lift_scatter_second(t):
            nc.vector.tensor_tensor(dt[t][:].indirect(n2_t[:]), over[t][:], pos_half[t][:], ALU.add)

        def weigh_z(t):
            nc.scalar.activation(
                z_dealt[:, t, :].rearrange("p (u m) -> p m u", u=PACK),
                dt[t][:].rearrange("p (m u) -> p m u", u=PACK),
                ACT.Copy,
                scale=g_cols[:, t : t + 1],
            )

        for t in range(PACK):
            lift_gather_first(t)

        wb_bf = [sb([P, HALF * PACK], BF16, "wb_bf%d" % h) for h in range(2)]
        wb_codes = sb([P, N], U32, "wb_codes")
        wb_scales = sb([P, N], U8, "wb_scales")
        for h in range(2):
            nc.scalar.copy(woven(wb_bf[h][:]), planes(wb_raw[:, :, cols(h)]))

        g_ps = bank(PACK)
        nc.tensor.transpose(g_ps[:, 0:P], g_rows[:], ident[:])
        g_cols = sb([P, 2 * PACK], F32, "g_cols")
        nc.scalar.copy(g_cols[:], g_ps[:, 0 : 2 * PACK])
        gi_neg = sb([P, PACK], F32, "gi_neg")
        nc.scalar.activation(gi_neg[:], g_ps[:, PACK : 2 * PACK], ACT.Copy, scale=-1.0)
        gi_safe = sb([P, PACK], F32, "gi_safe")
        gi_inv = sb([P, PACK], F32, "gi_inv")

        for t in range(PACK):
            lift_gather_second(t)

        lift_scatter_first(0)
        for h in range(2):
            quantise(wb_codes[:, cols(h)], wb_scales[:, cols(h)], wb_bf[h][:])
        nc.vector.scalar_tensor_tensor(
            gi_safe[:], g_cols[:, PACK : 2 * PACK], 0.0, g_cols[:, PACK : 2 * PACK], ALU.is_equal, ALU.add
        )
        lift_scatter_second(0)
        lift_scatter_first(1, "wb_bf1")
        nc.vector.reciprocal(gi_inv[:], gi_safe[:])
        lift_scatter_second(1)

        rows = [sb([P, 2 * N], F32, "rows%d" % t) for t in range(PACK)]
        b_plain = [rows[t ^ 1][:, N : 2 * N] for t in range(PACK)]
        for t in range(PACK):
            acc = bank(PACK + t)
            tok = slice(t * P, (t + 1) * P)
            product(acc[:], xb_words[:, tok], xb_scales[:, tok], wb_codes[:], wb_scales[:])
            nc.scalar.activation(rows[t][:, 0:N], acc[:], ACT.Copy, scale=gi_neg[:, t : t + 1])
            nc.scalar.activation(b_plain[t], acc[:], ACT.Copy, scale=gi_neg[:, t : t + 1])

        weigh_z(0)
        weigh_z(1)

        gap = [sb([P, N], F32, "gap%d" % t) for t in range(PACK)]
        dist = sb([P, PACK, N], F32, "dist")
        root = sb([P, PACK, N], F32, "root")
        inv_den = sb([P, PACK, N], F32, "inv_den")
        num = sb([P, PACK, N], F32, "num")
        for t in range(PACK):
            nc.vector.tensor_tensor(gap[t][:], rows[t][:].indirect(n4_t[:]), b_plain[t], ALU.subtract)
            nc.scalar.activation(dist[:, t, :], gap[t][:], ACT.Abs, scale=gi_inv[:, t : t + 1])
            nc.scalar.activation(root[:, t, :], dist[:, t, :], ACT.Abs_reciprocal_sqrt, bias=0.5)
            nc.scalar.activation(inv_den[:, t, :], root[:, t, :], ACT.Square)
            nc.vector.tensor_tensor(num[:, t, :], rows[t][:].indirect(n3_t[:]), b_plain[t], ALU.subtract)

        lift_scatter_first(2, "gap2")
        lift_scatter_first(3, "gap3")
        for t in (2, 3):
            lift_scatter_second(t)
            weigh_z(t)

        z_bf = [sb([P, P * PACK], BF16, "z_bf%d" % u) for u in range(PACK)]
        z_codes = sb([P, H], U32, "z_codes")
        z_scales = sb([P, H], U8, "z_scales")
        for u in range(PACK):
            nc.scalar.copy(woven(z_bf[u][:]), planes(z_dealt[:, :, u * P : (u + 1) * P]))

        z2_bf = [sb([P, HALF * PACK], BF16, "z2_bf%d" % h) for h in range(2)]
        for h in range(2):
            nc.vector.tensor_tensor(
                woven(z2_bf[h][:], 2), planes(num[:, :, cols(h)], 2), planes(inv_den[:, :, cols(h)], 2), ALU.mult
            )
        z2_scales = sb([P, N], U8, "z2_scales")

        def quantise_z(u):
            feat = slice(u * P, (u + 1) * P)
            quantise(z_codes[:, feat], z_scales[:, feat], z_bf[u][:])

        z2_codes = [sb([P, HALF], U32, "z2_codes0")]
        quantise(z2_codes[0][:], z2_scales[:, cols(0)], z2_bf[0][:])
        quantise_z(0)
        z2_codes.append(sb([P, HALF], U32, "z2_codes1", "z_bf0"))
        quantise(z2_codes[1][:], z2_scales[:, cols(1)], z2_bf[1][:])
        for u in range(1, PACK):
            quantise_z(u)

        sums = {}
        for u in range(PACK):
            feat = slice(u * P, (u + 1) * P)
            for h in range(2):
                acc = bank(h * PACK + u)
                sums[u, h] = acc
                product(acc[:, 0:HALF], z_codes[:, feat], z_scales[:, feat], z2_codes[h][:], z2_scales[:, cols(h)])
                nc.scalar.activation(rows[u][:, cols(h)], acc[:, 0:HALF], ACT.Copy, scale=0.0625)

        at5 = sb([P, PACK, N], F32, "at5")
        at6 = sb([P, PACK, N], F32, "at6")
        larger = sb([P, PACK, N], F32, "larger")
        result = sb([P, PACK, N], F32, "result")
        out_bf = [sb([P, HALF * PACK], BF16, "out_bf%d" % h) for h in range(2)]
        out_codes = sb([P, N], I32, "out_codes")
        out_scales = sb([P, N], U8, "out_scales")
        out_rows = out_0.rearrange("(p u) c -> p u c", u=PACK)
        out_words = out_1[0].rearrange("p n t -> p (n t)").bitcast(I32)

        def fetch(dst, lst, u, span):
            nc.vector.tensor_copy(dst[:, u, span], rows[u][:].indirect(lst[:, span.start // PER_COL : span.stop // PER_COL]))

        def take_larger(u, h):
            nc.vector.scalar_tensor_tensor(
                larger[:, u, cols(h)], sums[u, h][:, 0:HALF], 0.0625, at5[:, u, cols(h)], ALU.mult, ALU.max
            )

        def finish(u, span):
            nc.vector.tensor_tensor(result[:, u, span], larger[:, u, span], at6[:, u, span], ALU.min)
            nc.sync.dma_start(out_rows[:, u, span], result[:, u, span])

        def finish_aside(u):
            above = sb([P, N], F32, "above%d" % u)
            cut = sb([P, N], F32, "cut%d" % u)
            nc.gpsimd.tensor_tensor(above[:], larger[:, u, :], at6[:, u, :], ALU.subtract)
            nc.scalar.activation(cut[:], above[:], ACT.Relu)
            nc.gpsimd.tensor_tensor(result[:, u, :], larger[:, u, :], cut[:], ALU.subtract)
            nc.sync.dma_start(out_rows[:, u, :], result[:, u, :])

        whole = slice(0, N)
        for u in range(PACK - 1):
            fetch(at5, n5_t, u, whole)
            fetch(at6, n6_t, u, whole)
            for h in range(2):
                take_larger(u, h)
            if u < 2:
                finish_aside(u)
        last = PACK - 1
        fetch(at5, n5_t, last, cols(0))
        fetch(at6, n6_t, last, cols(0))
        take_larger(last, 0)
        finish(last - 1, whole)
        fetch(at5, n5_t, last, cols(1))
        finish(last, cols(0))
        fetch(at6, n6_t, last, cols(1))
        take_larger(last, 1)
        nc.scalar.copy(woven(out_bf[0][:]), planes(result[:, :, cols(0)]))
        finish(last, cols(1))
        nc.vector.tensor_copy(woven(out_bf[1][:]), planes(result[:, :, cols(1)]))
        for h in range(2):
            quantise(out_codes[:, cols(h)], out_scales[:, cols(h)], out_bf[h][:])
            nc.sync.dma_start(out_words[:, cols(h)], out_codes[:, cols(h)])
        for q in range(4):
            queue = nc.scalar if q % 2 == 0 else nc.sync
            queue.dma_start(
                out_2[0, 4 * q : 4 * q + 4, :].bitcast(I32), out_scales[32 * q : 32 * q + 4, :].bitcast(I32)
            )
